import numpy as np, ml_dtypes
CORES = [0,1,2,3]
N = 4
def setup_inputs(rng):
    return {"x1": rng.standard_normal((N, 128, 1024), dtype=np.float32), "x2": rng.standard_normal((N, 128, 64), dtype=np.float32).astype(ml_dtypes.bfloat16)}
def reference(x1, x2):
    out = []
    s = x1.sum(axis=0, dtype=np.float64).astype(x1.dtype)
    b = 1024 // N
    out.append(np.stack([s[:, r * b:(r + 1) * b] for r in range(N)]))
    out.append(np.broadcast_to(x2[2], x2.shape))
    return {"y1": out[0], "y2": out[1]}

@@ -1,0 +1,72 @@
+from concourse.bass import DstId, RemoteDMATransfer
+from concourse.mybir import AluOpType
+
+N = 4
+B = 256
+ROOT = 2
+
+SCRATCH = {
+    "xs": ("sbuf", [128, N * B], "float32"),
+    "land": ("sbuf", [128, (N - 1) * B], "float32"),
+    "bc": ("sbuf", [128, 64], "bfloat16"),
+}
+SEMAPHORES = ["ld1", "ld2", "seed", "acc_a", "acc_b", "st2", "sent", "got1", "got2"]
+
+SCATTER_MASKS = (0x000F, 0x00F0, 0x0F00)
+SCATTER_ENGINES = 4
+BCAST_MASK = 0xFFFF
+BCAST_ENGINES = 16
+
+
+def rank_program(g, core, T, topo):
+    r = T.rank_of(core)
+    if r is None:
+        return
+    S = T.sem
+
+    def dst_id(rank):
+        rid, pid, _se = topo.addr(T.cores[rank])
+        return DstId(rid=rid, pnc=pid)
+
+    def slot(k):
+        return T.land[:, k * B:(k + 1) * B]
+
+    others = [d for d in range(N) if d != r]
+    sent = 0
+
+    if r == ROOT:
+        g.dma_start(T.bc[:], T.x2[:]).then_inc(S.ld2, 16)
+        g.dma_start(T.y2[:], T.x2[:]).then_inc(S.st2, 16)
+    g.dma_start(T.xs[:], T.x1[:]).then_inc(S.ld1, 16)
+    g.dma_start(T.y1[:], T.x1[:, r * B:(r + 1) * B]).then_inc(S.seed, 16)
+
+    if r == ROOT:
+        g.wait_ge(S.ld2, 16)
+        g.remote_dma_fused(
+            [RemoteDMATransfer(dst_ids=[dst_id(d) for d in others], dma_engine_mask=BCAST_MASK, remote_sem=S.got2,
+                               srcs=[T.bc[:]], dsts=[T.bc[:] for _d in others], alu_op=0)],
+            local_sem=S.sent)
+        sent += BCAST_ENGINES
+
+    g.wait_ge(S.ld1, 16)
+    g.remote_dma_fused(
+        [RemoteDMATransfer(dst_ids=[dst_id(d)], dma_engine_mask=SCATTER_MASKS[i], remote_sem=S.got1,
+                           src=T.xs[:, d * B:(d + 1) * B], dst=slot((r - d - 1) % N), alu_op=0)
+         for i, d in enumerate(others)],
+        local_sem=S.sent)
+    sent += SCATTER_ENGINES * len(others)
+
+    if r != ROOT:
+        g.wait_ge(S.got2, BCAST_ENGINES)
+        g.dma_start(T.y2[:], T.bc[:]).then_inc(S.st2, 16)
+
+    g.wait_ge(S.got1, SCATTER_ENGINES * len(others))
+    g.dma_start(slot(0), slot(1), accum_op=AluOpType.add).then_inc(S.acc_a, 16)
+    g.wait_ge(S.seed, 16)
+    g.dma_start(T.y1[:], slot(2), accum_op=AluOpType.add).then_inc(S.acc_a, 16)
+    g.wait_ge(S.acc_a, 32)
+    g.dma_start(T.y1[:], slot(0), accum_op=AluOpType.add).then_inc(S.acc_b, 16)
+
+    g.wait_ge(S.acc_b, 16)
+    g.wait_ge(S.st2, 16)
+    g.wait_ge(S.sent, sent)

@@ -25,7 +25,7 @@ def rank_program(g, core, T, topo):
     S = T.sem
 
     def dst_id(rank):
-        rid, pid, _se = topo.addr(T.cores[rank])
+        rid, pid, sengine = topo.addr(T.cores[rank])
         return DstId(rid=rid, pnc=pid)
 
     def slot(k):
@@ -37,14 +37,15 @@ def rank_program(g, core, T, topo):
     if r == ROOT:
         g.dma_start(T.bc[:], T.x2[:]).then_inc(S.ld2, 16)
         g.dma_start(T.y2[:], T.x2[:]).then_inc(S.st2, 16)
-    g.dma_start(T.xs[:], T.x1[:]).then_inc(S.ld1, 16)
+    lo, hi = min(others) * B, (max(others) + 1) * B
+    g.dma_start(T.xs[:, lo:hi], T.x1[:, lo:hi]).then_inc(S.ld1, 16)
     g.dma_start(T.y1[:], T.x1[:, r * B:(r + 1) * B]).then_inc(S.seed, 16)
 
     if r == ROOT:
         g.wait_ge(S.ld2, 16)
         g.remote_dma_fused(
             [RemoteDMATransfer(dst_ids=[dst_id(d) for d in others], dma_engine_mask=BCAST_MASK, remote_sem=S.got2,
-                               srcs=[T.bc[:]], dsts=[T.bc[:] for _d in others], alu_op=0)],
+                               srcs=[T.bc[:]], dsts=[T.bc[:] for d in others], alu_op=0)],
             local_sem=S.sent)
         sent += BCAST_ENGINES
 

from concourse.bass import DstId, RemoteDMATransfer
from concourse.mybir import AluOpType

N = 4
B = 256
ROOT = 2

SCRATCH = {
    "xs": ("sbuf", [128, N * B], "float32"),
    "land": ("sbuf", [128, (N - 1) * B], "float32"),
    "bc": ("sbuf", [128, 64], "bfloat16"),
}
SEMAPHORES = ["ld1", "ld2", "seed", "acc_a", "acc_b", "st2", "sent", "got1", "got2"]

SCATTER_MASKS = (0x000F, 0x00F0, 0x0F00)
SCATTER_ENGINES = 4
BCAST_MASK = 0xFFFF
BCAST_ENGINES = 16


def rank_program(g, core, T, topo):
    r = T.rank_of(core)
    if r is None:
        return
    S = T.sem

    def dst_id(rank):
        rid, pid, sengine = topo.addr(T.cores[rank])
        return DstId(rid=rid, pnc=pid)

    def slot(k):
        return T.land[:, k * B:(k + 1) * B]

    others = [d for d in range(N) if d != r]
    sent = 0

    if r == ROOT:
        g.dma_start(T.bc[:], T.x2[:]).then_inc(S.ld2, 16)
        g.dma_start(T.y2[:], T.x2[:]).then_inc(S.st2, 16)
    lo, hi = min(others) * B, (max(others) + 1) * B
    g.dma_start(T.xs[:, lo:hi], T.x1[:, lo:hi]).then_inc(S.ld1, 16)
    g.dma_start(T.y1[:], T.x1[:, r * B:(r + 1) * B]).then_inc(S.seed, 16)

    if r == ROOT:
        g.wait_ge(S.ld2, 16)
        g.remote_dma_fused(
            [RemoteDMATransfer(dst_ids=[dst_id(d) for d in others], dma_engine_mask=BCAST_MASK, remote_sem=S.got2,
                               srcs=[T.bc[:]], dsts=[T.bc[:] for d in others], alu_op=0)],
            local_sem=S.sent)
        sent += BCAST_ENGINES

    g.wait_ge(S.ld1, 16)
    g.remote_dma_fused(
        [RemoteDMATransfer(dst_ids=[dst_id(d)], dma_engine_mask=SCATTER_MASKS[i], remote_sem=S.got1,
                           src=T.xs[:, d * B:(d + 1) * B], dst=slot((r - d - 1) % N), alu_op=0)
         for i, d in enumerate(others)],
        local_sem=S.sent)
    sent += SCATTER_ENGINES * len(others)

    if r != ROOT:
        g.wait_ge(S.got2, BCAST_ENGINES)
        g.dma_start(T.y2[:], T.bc[:]).then_inc(S.st2, 16)

    g.wait_ge(S.got1, SCATTER_ENGINES * len(others))
    g.dma_start(slot(0), slot(1), accum_op=AluOpType.add).then_inc(S.acc_a, 16)
    g.wait_ge(S.seed, 16)
    g.dma_start(T.y1[:], slot(2), accum_op=AluOpType.add).then_inc(S.acc_a, 16)
    g.wait_ge(S.acc_a, 32)
    g.dma_start(T.y1[:], slot(0), accum_op=AluOpType.add).then_inc(S.acc_b, 16)

    g.wait_ge(S.acc_b, 16)
    g.wait_ge(S.st2, 16)
    g.wait_ge(S.sent, sent)
